import numpy as np
import ml_dtypes

BF16 = ml_dtypes.bfloat16


def bf(x):
    return np.asarray(x, np.float32).astype(BF16)


def f32(x):
    return np.asarray(x, np.float32)


def f64(x):
    return np.asarray(x).astype(np.float64)


def striped(idx):
    return np.tile(idx.reshape(-1, 16).T, (8, 1))


S, K, M, N, E, Q, V, D = 512, 128, 512, 192, 2, 96, 128, 4


def setup_inputs():
    return {"base": bf(np.random.standard_normal((M, S))), "x": bf(np.random.standard_normal((K, N))), "w": bf(1.5 * np.random.standard_normal((E, K, M)) / np.sqrt(K)), "offs": striped(np.random.permutation(S)[:N])}


def reference(base, x, w, offs):
    idx = offs[:16].T.reshape(-1)
    z = f64(base).copy()
    for e in range(E):
        z[:, idx[e * Q : (e + 1) * Q]] += f64(w)[e].T @ f64(x)[:, e * Q : (e + 1) * Q]
    z = z
    return z.reshape(M, V, D).max(axis=2)

@@ -1,0 +1,60 @@
+import concourse.mybir as mybir
+from concourse.masks import make_identity
+
+BF16, F32, U16 = mybir.dt.bfloat16, mybir.dt.float32, mybir.dt.uint16
+
+P = 128
+M = 512
+S = 512
+N = 192
+SENSORS = 2
+PIECE = N // SENSORS
+POOL = 4
+V = S // POOL
+BLOCKS = M // P
+LANES = 16
+
+FLOPS = 2 * P * M * N
+
+
+def tile_rows_unpool_max_none_kernel(tc, base, x, w, offs, out):
+    nc = tc.nc
+    base_rows = base.rearrange("(a p) s -> a p s", p=P)
+    out_rows = out.rearrange("(a p) v -> a p v", p=P)
+    with (
+        tc.tile_pool(name="held", bufs=1) as held,
+        tc.psum_pool(name="windows", bufs=1) as windows,
+    ):
+        base_tiles = [held.tile([P, S], BF16, name=f"base{a}") for a in range(BLOCKS)]
+        for a in range(BLOCKS):
+            nc.sync.dma_start(base_tiles[a][:], base_rows[a])
+        offsets = held.tile([P, N // LANES], U16, name="offsets")
+        nc.sync.dma_start(offsets[:], offs)
+        points = held.tile([P, N], BF16, name="points")
+        nc.scalar.dma_start(points[:], x)
+        weights = held.tile([P, SENSORS, M], BF16, name="weights")
+        nc.scalar.dma_start(weights[:], w.rearrange("e k m -> k e m"))
+
+        identity = held.tile([P, P], BF16, name="identity")
+        make_identity(nc, identity[:])
+
+        z = [windows.tile([P, S], F32, name=f"z{a}") for a in range(BLOCKS)]
+        for a in range(BLOCKS):
+            nc.tensor.matmul(z[a][:], identity[:], base_tiles[a][:], start=True, stop=False)
+
+        for a in range(BLOCKS):
+            for e in range(SENSORS):
+                columns = offsets[:, e * (PIECE // LANES) : (e + 1) * (PIECE // LANES)]
+                nc.tensor.matmul(
+                    z[a][:].indirect(columns),
+                    weights[:, e, a * P : (a + 1) * P],
+                    points[:, e * PIECE : (e + 1) * PIECE],
+                    start=False,
+                    stop=(e == SENSORS - 1),
+                )
+
+        for a in range(BLOCKS):
+            pooled = held.tile([P, V], F32, name=f"pooled{a}")
+            cells = z[a][:].rearrange("p (v d) -> p v d", d=POOL)
+            nc.vector.tensor_reduce(pooled[:], cells, mybir.AxisListType.X, mybir.AluOpType.max)
+            nc.sync.dma_start(out_rows[a], pooled[:])

@@ -12,6 +12,9 @@ PIECE = N // SENSORS
 POOL = 4
 V = S // POOL
 BLOCKS = M // P
+HALVES = 2
+HALF = BLOCKS // HALVES
+FILL_PIECES = (1, 16)
 LANES = 16
 
 FLOPS = 2 * P * M * N
@@ -20,41 +23,56 @@ FLOPS = 2 * P * M * N
 def tile_rows_unpool_max_none_kernel(tc, base, x, w, offs, out):
     nc = tc.nc
     base_rows = base.rearrange("(a p) s -> a p s", p=P)
+    w_halves = w.rearrange("e k (h m) -> h k e m", h=HALVES)
     out_rows = out.rearrange("(a p) v -> a p v", p=P)
     with (
         tc.tile_pool(name="held", bufs=1) as held,
         tc.psum_pool(name="windows", bufs=1) as windows,
     ):
         base_tiles = [held.tile([P, S], BF16, name=f"base{a}") for a in range(BLOCKS)]
-        for a in range(BLOCKS):
-            nc.sync.dma_start(base_tiles[a][:], base_rows[a])
-        offsets = held.tile([P, N // LANES], U16, name="offsets")
-        nc.sync.dma_start(offsets[:], offs)
+        w_tiles = [held.tile([P, SENSORS, HALF * P], BF16, name=f"w{h}") for h in range(HALVES)]
         points = held.tile([P, N], BF16, name="points")
+        offsets = held.tile([P, N // LANES], U16, name="offsets")
         nc.scalar.dma_start(points[:], x)
-        weights = held.tile([P, SENSORS, M], BF16, name="weights")
-        nc.scalar.dma_start(weights[:], w.rearrange("e k m -> k e m"))
+        for h in range(HALVES):
+            for a in range(h * HALF, (h + 1) * HALF):
+                nc.sync.dma_start(base_tiles[a][:], base_rows[a])
+            if h == 0:
+                nc.sync.dma_start(offsets[:], offs)
+            nc.scalar.dma_start(w_tiles[h][:], w_halves[h])
+
+        zeros = held.tile([P, P], BF16, name="zeros")
+        nc.gpsimd.memset(zeros[:], 0.0)
+        z = [windows.tile([P, S], F32, name=f"z{a}") for a in range(BLOCKS)]
+        for a in range(BLOCKS):
+            chunks = z[a][:].rearrange("p (r c) -> p r c", c=P)
+            nc.tensor.matmul(chunks, zeros[:], zeros[:].unsqueeze(1).to_broadcast([P, S // P, P]), start=True, stop=False)
 
         identity = held.tile([P, P], BF16, name="identity")
         make_identity(nc, identity[:])
 
-        z = [windows.tile([P, S], F32, name=f"z{a}") for a in range(BLOCKS)]
-        for a in range(BLOCKS):
-            nc.tensor.matmul(z[a][:], identity[:], base_tiles[a][:], start=True, stop=False)
+        for h in range(HALVES):
+            blocks = range(h * HALF, (h + 1) * HALF)
 
-        for a in range(BLOCKS):
-            for e in range(SENSORS):
-                columns = offsets[:, e * (PIECE // LANES) : (e + 1) * (PIECE // LANES)]
-                nc.tensor.matmul(
-                    z[a][:].indirect(columns),
-                    weights[:, e, a * P : (a + 1) * P],
-                    points[:, e * PIECE : (e + 1) * PIECE],
-                    start=False,
-                    stop=(e == SENSORS - 1),
-                )
+            width = S // FILL_PIECES[h]
+            for a in blocks:
+                for c in range(0, S, width):
+                    nc.tensor.matmul(z[a][:, c : c + width], identity[:], base_tiles[a][:, c : c + width], start=False, stop=False)
 
-        for a in range(BLOCKS):
-            pooled = held.tile([P, V], F32, name=f"pooled{a}")
-            cells = z[a][:].rearrange("p (v d) -> p v d", d=POOL)
-            nc.vector.tensor_reduce(pooled[:], cells, mybir.AxisListType.X, mybir.AluOpType.max)
-            nc.sync.dma_start(out_rows[a], pooled[:])
+            for a in blocks:
+                within = a - h * HALF
+                for e in range(SENSORS):
+                    columns = offsets[:, e * (PIECE // LANES) : (e + 1) * (PIECE // LANES)]
+                    nc.tensor.matmul(
+                        z[a][:].indirect(columns),
+                        w_tiles[h][:, e, within * P : (within + 1) * P],
+                        points[:, e * PIECE : (e + 1) * PIECE],
+                        start=False,
+                        stop=(e == SENSORS - 1),
+                    )
+
+            for a in blocks:
+                pooled = held.tile([P, V], F32, name=f"pooled{a}")
+                cells = z[a][:].rearrange("p (v d) -> p v d", d=POOL)
+                nc.vector.tensor_reduce(pooled[:], cells, mybir.AxisListType.X, mybir.AluOpType.max)
+                nc.sync.dma_start(out_rows[a], pooled[:])

@@ -14,7 +14,7 @@ V = S // POOL
 BLOCKS = M // P
 HALVES = 2
 HALF = BLOCKS // HALVES
-FILL_PIECES = (1, 16)
+FILL_WIDTHS = (S, S, 32, 64)
 LANES = 16
 
 FLOPS = 2 * P * M * N
@@ -33,13 +33,13 @@ def tile_rows_unpool_max_none_kernel(tc, base, x, w, offs, out):
         w_tiles = [held.tile([P, SENSORS, HALF * P], BF16, name=f"w{h}") for h in range(HALVES)]
         points = held.tile([P, N], BF16, name="points")
         offsets = held.tile([P, N // LANES], U16, name="offsets")
-        nc.scalar.dma_start(points[:], x)
         for h in range(HALVES):
             for a in range(h * HALF, (h + 1) * HALF):
                 nc.sync.dma_start(base_tiles[a][:], base_rows[a])
             if h == 0:
                 nc.sync.dma_start(offsets[:], offs)
-            nc.scalar.dma_start(w_tiles[h][:], w_halves[h])
+                nc.sync.dma_start(points[:], x)
+            nc.sync.dma_start(w_tiles[h][:], w_halves[h])
 
         zeros = held.tile([P, P], BF16, name="zeros")
         nc.gpsimd.memset(zeros[:], 0.0)
@@ -54,8 +54,8 @@ def tile_rows_unpool_max_none_kernel(tc, base, x, w, offs, out):
         for h in range(HALVES):
             blocks = range(h * HALF, (h + 1) * HALF)
 
-            width = S // FILL_PIECES[h]
             for a in blocks:
+                width = FILL_WIDTHS[a]
                 for c in range(0, S, width):
                     nc.tensor.matmul(z[a][:, c : c + width], identity[:], base_tiles[a][:, c : c + width], start=False, stop=False)
 

import concourse.mybir as mybir
from concourse.masks import make_identity

BF16, F32, U16 = mybir.dt.bfloat16, mybir.dt.float32, mybir.dt.uint16

P = 128
M = 512
S = 512
N = 192
SENSORS = 2
PIECE = N // SENSORS
POOL = 4
V = S // POOL
BLOCKS = M // P
HALVES = 2
HALF = BLOCKS // HALVES
FILL_WIDTHS = (S, S, 32, 64)
LANES = 16

FLOPS = 2 * P * M * N


def tile_rows_unpool_max_none_kernel(tc, base, x, w, offs, out):
    nc = tc.nc
    base_rows = base.rearrange("(a p) s -> a p s", p=P)
    w_halves = w.rearrange("e k (h m) -> h k e m", h=HALVES)
    out_rows = out.rearrange("(a p) v -> a p v", p=P)
    with (
        tc.tile_pool(name="held", bufs=1) as held,
        tc.psum_pool(name="windows", bufs=1) as windows,
    ):
        base_tiles = [held.tile([P, S], BF16, name=f"base{a}") for a in range(BLOCKS)]
        w_tiles = [held.tile([P, SENSORS, HALF * P], BF16, name=f"w{h}") for h in range(HALVES)]
        points = held.tile([P, N], BF16, name="points")
        offsets = held.tile([P, N // LANES], U16, name="offsets")
        for h in range(HALVES):
            for a in range(h * HALF, (h + 1) * HALF):
                nc.sync.dma_start(base_tiles[a][:], base_rows[a])
            if h == 0:
                nc.sync.dma_start(offsets[:], offs)
                nc.sync.dma_start(points[:], x)
            nc.sync.dma_start(w_tiles[h][:], w_halves[h])

        zeros = held.tile([P, P], BF16, name="zeros")
        nc.gpsimd.memset(zeros[:], 0.0)
        z = [windows.tile([P, S], F32, name=f"z{a}") for a in range(BLOCKS)]
        for a in range(BLOCKS):
            chunks = z[a][:].rearrange("p (r c) -> p r c", c=P)
            nc.tensor.matmul(chunks, zeros[:], zeros[:].unsqueeze(1).to_broadcast([P, S // P, P]), start=True, stop=False)

        identity = held.tile([P, P], BF16, name="identity")
        make_identity(nc, identity[:])

        for h in range(HALVES):
            blocks = range(h * HALF, (h + 1) * HALF)

            for a in blocks:
                width = FILL_WIDTHS[a]
                for c in range(0, S, width):
                    nc.tensor.matmul(z[a][:, c : c + width], identity[:], base_tiles[a][:, c : c + width], start=False, stop=False)

            for a in blocks:
                within = a - h * HALF
                for e in range(SENSORS):
                    columns = offsets[:, e * (PIECE // LANES) : (e + 1) * (PIECE // LANES)]
                    nc.tensor.matmul(
                        z[a][:].indirect(columns),
                        w_tiles[h][:, e, within * P : (within + 1) * P],
                        points[:, e * PIECE : (e + 1) * PIECE],
                        start=False,
                        stop=(e == SENSORS - 1),
                    )

            for a in blocks:
                pooled = held.tile([P, V], F32, name=f"pooled{a}")
                cells = z[a][:].rearrange("p (v d) -> p v d", d=POOL)
                nc.vector.tensor_reduce(pooled[:], cells, mybir.AxisListType.X, mybir.AluOpType.max)
                nc.sync.dma_start(out_rows[a], pooled[:])
